import numpy as np
import ml_dtypes


def mxq(x, axis, fmt="e4m3"):
    dtype, down = {"e4m3": (ml_dtypes.float8_e4m3fn, 7), "e5m2": (ml_dtypes.float8_e5m2, 14)}[fmt]
    v = np.moveaxis(np.asarray(x, np.float32).astype(ml_dtypes.bfloat16).astype(np.float64), axis, -1)
    blocks = v.reshape(v.shape[:-1] + (-1, 32))
    amax = np.abs(blocks).max(-1, keepdims=True)
    byte = np.maximum(np.where(amax > 0, np.frexp(amax)[1] - 1 + 127, 0) - down, 1)
    scale = np.exp2(byte - 127.0)
    codes = (blocks / scale).astype(np.float32).astype(dtype).astype(np.float64)
    return np.moveaxis((codes * scale).reshape(v.shape), -1, axis)


WIDE = False


def mx_kscale(k):
    if not WIDE:
        return np.ones(k)
    levels = np.array([10, -10, 5, -5, 0])
    if k % 512:
        return np.exp2(np.random.permutation(np.resize(levels, k // 32))).repeat(32)
    a = np.empty((k // 512, 16))
    for p in range(k // 512):
        a[p, :8] = np.random.permutation(np.resize(levels, 8))
        for g in range(8):
            far = levels[np.abs(levels - a[p, g]) >= 10]
            a[p, g + 8] = far[np.random.randint(len(far))]
    return np.exp2(a.ravel()).repeat(32)


def f64(x):
    return np.asarray(x).astype(np.float64)


def striped(idx):
    return np.tile(idx.reshape(-1, 16).T, (8, 1)).astype(np.uint16)


def unstriped(offs):
    return offs[:16].T.reshape(-1).astype(np.int64)


def striped8(idx):
    return np.concatenate([x.reshape(-1, 16).T for x in idx]).astype(np.uint16)


def runs(offs, k):
    lists = np.stack([offs[16 * r : 16 * r + 16].T.reshape(-1) for r in range(8)]).astype(np.int64)
    return lists[np.arange(k) % 512 // 64]


def pack_weight(w):
    k, n = w.shape
    w = f64(np.asarray(w, np.float32).astype(ml_dtypes.bfloat16)).reshape(k // 32, 32, n)
    amax = np.abs(w).max(1)
    byte = np.clip(np.where(amax > 0, np.frexp(amax)[1] - 1 + 127 - 7, 1), 1, 254)
    scaled = (w * np.exp2(127.0 - byte)[:, None, :]).reshape(k, n).astype(np.float32)
    words = np.ascontiguousarray(scaled.reshape(k // 512, 128, 4, n).transpose(0, 1, 3, 2)).astype(ml_dtypes.float8_e4m3fn).view(np.uint8)
    return words, np.ascontiguousarray(byte.astype(np.uint8).reshape(k // 512, 16, n))


def unpack_weight(words, scales):
    g, p, n, _ = words.shape
    vals = np.ascontiguousarray(words).view(ml_dtypes.float8_e4m3fn).astype(np.float64) * np.repeat(np.exp2(scales.astype(np.float64) - 127.0), 8, axis=1)[..., None]
    return vals.transpose(0, 1, 3, 2).reshape(g * 512, n)


def sigmoid(v):
    return 1.0 / (1.0 + np.exp(-np.maximum(v, -700.0)))


K, T, S, N, H, G = 512, 2048, 512, 512, 512, 2048


def setup_inputs():
    n = np.random.standard_normal
    s = mx_kscale(K)[:, None]
    u = mx_kscale(S)
    packed_xT = pack_weight(n((K, T)) * s)
    packed_dT = pack_weight(n((K, G)) / s)
    return {
        "x_words": packed_xT[0],
        "x_scales": packed_xT[1],
        "w1": (n((K, H)) / np.sqrt(K) / s).astype(np.float32),
        "gn": (np.random.uniform(0.5, 1.5, (H, 1)) * u[:, None]).astype(np.float32),
        "w2": (n((H, N)) / np.sqrt(H) / u[:, None]).astype(np.float32),
        "d_words": packed_dT[0],
        "d_scales": packed_dT[1],
        "offs": striped(np.random.permutation(T)[:S]),
        "n1": striped8(np.stack([np.random.permutation(S) for _ in range(8)])),
        "n2": striped8(np.stack([np.random.permutation(S) for _ in range(8)])),
        "two": striped(np.random.permutation(T)[:S]),
        "k1": striped8(np.random.randint(0, G, (8, H))),
        "n3": striped(np.random.permutation(S)),
        "n4": striped(np.random.permutation(S)),
    }


def reference(x_words, x_scales, w1, gn, w2, d_words, d_scales, offs, n1, n2, two, k1, n3, n4):
    xq = unpack_weight(x_words, x_scales)[:, unstriped(offs)]
    y = mxq(f64(w1), 0, "e4m3").T @ xq
    pa = y[np.arange(H)[:, None], runs(n1, H)]
    pb = y[np.arange(H)[:, None], runs(n2, H)]
    z = f64(gn) * (np.maximum(np.maximum(y, pa), pb) - (0.5 * (np.minimum(np.minimum(y, pa), pb))))
    a = mxq(f64(w2), 0, "e4m3").T @ mxq(z, 0, "e4m3")
    d_k1 = unpack_weight(d_words, d_scales)[np.arange(K)[:, None], runs(k1, K)]
    x_two = unpack_weight(x_words, x_scales)[:, unstriped(two)]
    b = 0.0625 * (d_k1.T @ x_two)
    return a * (sigmoid(b[:, unstriped(n4)])) - (0.5 * a[:, unstriped(n3)])

@@ -1,0 +1,221 @@
+from contextlib import ExitStack
+
+import concourse.mybir as mybir
+
+F32 = mybir.dt.float32
+BF16 = mybir.dt.bfloat16
+I32 = mybir.dt.int32
+U32 = mybir.dt.uint32
+U16 = mybir.dt.uint16
+U8 = mybir.dt.uint8
+FP8X4 = mybir.dt.float8_e4m3fn_x4
+ACT = mybir.ActivationFunctionType
+ALU = mybir.AluOpType
+
+P = 128
+PACK = 4
+S = 512
+TABLE = 2048
+HALF = S // 2
+TILES = 4
+FLOPS = 3 * 2 * 512 * 512 * 512
+
+
+def tile_picked_cdjoingatebrange_none_p_kernel(
+    tc, x_words, x_scales, w1, gn, w2, d_words, d_scales, offs, n1, n2, two, k1, n3, n4, out
+):
+    nc = tc.nc
+    with ExitStack() as ctx:
+        lists = ctx.enter_context(tc.tile_pool(name="lists", bufs=1))
+        keep = ctx.enter_context(tc.tile_pool(name="keep", bufs=1))
+        psum = ctx.enter_context(tc.psum_pool(name="psum", bufs=1))
+
+        def load_list(name, src):
+            tile = lists.tile([P, S // 16], U16, name=name)
+            nc.sync.dma_start(tile[:], src)
+            return tile
+
+        def half_of(list_tile, h):
+            return list_tile[:, h * (HALF // 16) : (h + 1) * (HALF // 16)]
+
+        def cols(h):
+            return slice(h * HALF, (h + 1) * HALF)
+
+        def mx_tile(name, dtype, width):
+            return keep.tile([P, width], dtype, name=name, align_bytes=64)
+
+        xw = mx_tile("xw", U32, TABLE)
+        xs = mx_tile("xs", U8, TABLE)
+        dw = mx_tile("dw", U32, TABLE)
+        ds = mx_tile("ds", U8, TABLE)
+        d_plane = mx_tile("d_plane", U8, S)
+        nc.vector.memset(xs[:].bitcast(I32), 0)
+        nc.vector.memset(ds[:].bitcast(I32), 0)
+        nc.vector.memset(d_plane[:].bitcast(I32), 0)
+
+        offs_t = load_list("offs_t", offs)
+        nc.sync.dma_start(xw[:].bitcast(I32), x_words[0].rearrange("p n t -> p (n t)").bitcast(I32))
+        for q in range(4):
+            nc.sync.dma_start(xs[32 * q : 32 * q + 4, :].bitcast(I32), x_scales[0, 4 * q : 4 * q + 4, :].bitcast(I32))
+        w1_rows = w1.rearrange("(p j) c -> p j c", j=PACK)
+        w1_raw = []
+        for h in range(2):
+            part = keep.tile([P, PACK, HALF], F32, name="w1_raw%d" % h)
+            nc.sync.dma_start(part[:], w1_rows[:, :, cols(h)])
+            w1_raw.append(part)
+        two_t = load_list("two_t", two)
+        w2_raw = keep.tile([P, PACK, S], F32, name="w2_raw")
+        nc.sync.dma_start(w2_raw[:], w2.rearrange("(p j) c -> p j c", j=PACK))
+        n1_t = load_list("n1_t", n1)
+        n2_t = load_list("n2_t", n2)
+        k1_t = load_list("k1_t", k1)
+        nc.sync.dma_start(dw[:].bitcast(I32), d_words[0].rearrange("p n t -> p (n t)").bitcast(I32))
+        for e in range(2):
+            nc.sync.dma_start(ds[e:P:16, :].bitcast(I32), d_scales[0, e:16:2, :].bitcast(I32))
+        gain = keep.tile([P, PACK], F32, name="gain")
+        nc.sync.dma_start(gain[:], gn.rearrange("(p t) o -> p (t o)", t=PACK))
+        n4_t = load_list("n4_t", n4)
+        n3_t = load_list("n3_t", n3)
+
+        xo_w = mx_tile("xo_w", U32, S)
+        xo_s = mx_tile("xo_s", U8, S)
+        nc.vector.tensor_copy(xo_w[:], xw[:].indirect(offs_t[:]))
+        nc.vector.tensor_copy(xo_s[:], xs[:].indirect(offs_t[:]))
+
+        w1_bf = mx_tile("w1_bf", BF16, PACK * S)
+        w1_dealt = w1_bf[:].rearrange("p (t m j) -> p m j t", t=TILES, j=PACK)
+        for h in range(2):
+            nc.scalar.activation(
+                w1_dealt[:, 64 * h : 64 * (h + 1)],
+                w1_raw[h][:].rearrange("p j (m t) -> p m j t", t=TILES),
+                ACT.Copy,
+            )
+
+        xt_w = mx_tile("xt_w", U32, S)
+        xt_s = mx_tile("xt_s", U8, S)
+        nc.vector.tensor_copy(xt_w[:], xw[:].indirect(two_t[:]))
+
+        w1_w = mx_tile("w1_w", U32, S)
+        w1_s = mx_tile("w1_s", U8, S)
+        y_ps = []
+        for t in range(TILES):
+            blk = slice(t * P, (t + 1) * P)
+            nc.vector.quantize_mx(w1_w[:, blk].bitcast(FP8X4), w1_s[:, blk], w1_bf[:, t * S : (t + 1) * S])
+            bank = psum.tile([P, S], F32, name="y_ps%d" % t, tag="ya%d" % t)
+            nc.tensor.matmul_mx(bank[:], w1_w[:, blk].bitcast(FP8X4), w1_s[:, blk], xo_w[:].bitcast(FP8X4), xo_s[:], start=True, stop=True)
+            y_ps.append(bank)
+
+        nc.vector.tensor_copy(xt_s[:], xs[:].indirect(two_t[:]))
+
+        y = [keep.tile([P, S], F32, name="y%d" % t) for t in range(TILES)]
+        pa = [[keep.tile([P, HALF], F32, name="pa%d_%d" % (h, t)) for t in range(TILES)] for h in range(2)]
+        pb = [[keep.tile([P, HALF], F32, name="pb%d_%d" % (h, t)) for t in range(TILES)] for h in range(2)]
+        for h in range(2):
+            for t in range(TILES):
+                if h == 0:
+                    nc.scalar.activation(y[t][:], y_ps[t][:], ACT.Copy)
+                nc.scalar.activation(pa[h][t][:], y[t][:].indirect(half_of(n1_t, h)), ACT.Copy)
+                nc.scalar.activation(pb[h][t][:], y[t][:].indirect(half_of(n2_t, h)), ACT.Copy)
+
+        w2_bf = mx_tile("w2_bf", BF16, PACK * S)
+        w2_w = mx_tile("w2_w", U32, S)
+        w2_s = mx_tile("w2_s", U8, S)
+        nc.vector.tensor_copy(
+            w2_bf[:].rearrange("p (c i j) -> p c j i", i=4, j=PACK),
+            w2_raw[:].rearrange("p j (c i) -> p c j i", i=4),
+        )
+        dk_w = mx_tile("dk_w", U32, S)
+        dk_s = mx_tile("dk_s", U8, S)
+        nc.vector.tensor_copy(dk_s[:], ds[:].indirect(k1_t[:]))
+        nc.vector.quantize_mx(w2_w[:].bitcast(FP8X4), w2_s[:], w2_bf[:])
+        nc.vector.tensor_copy(dk_w[:], dw[:].indirect(k1_t[:]))
+        for s in range(4):
+            src = 16 * (s // 2) + s % 2
+            nc.sync.dma_start(d_plane[s:P:32, :].bitcast(I32), dk_s[src:P:32, :].bitcast(I32))
+
+        gate = []
+        for m in range(TILES):
+            blk = slice(m * P, (m + 1) * P)
+            bank = psum.tile([P, S], F32, name="b_ps%d" % m, tag="b%d" % m)
+            nc.tensor.matmul_mx(bank[:], dk_w[:, blk].bitcast(FP8X4), d_plane[:, blk], xt_w[:].bitcast(FP8X4), xt_s[:], start=True, stop=True)
+            th = keep.tile([P, S], F32, name="th%d" % m)
+            nc.scalar.activation(th[:], bank[:], ACT.Tanh, scale=0.03125)
+            g = keep.tile([P, S], F32, name="gate%d" % m)
+            for h in range(2):
+                nc.scalar.activation(g[:, cols(h)], th[:].indirect(half_of(n4_t, h)), ACT.Copy)
+            gate.append(g)
+
+        hi = [[keep.tile([P, HALF], F32, name="hi%d_%d" % (h, t)) for t in range(TILES)] for h in range(2)]
+        lo = [[keep.tile([P, HALF], F32, name="lo%d_%d" % (h, t)) for t in range(TILES)] for h in range(2)]
+        spread = [keep.tile([P, TILES, HALF], F32, name="spread%d" % h) for h in range(2)]
+        z_bf = [mx_tile("z_bf%d" % h, BF16, PACK * HALF) for h in range(2)]
+        z_w = [mx_tile("z_w%d" % h, U32, HALF) for h in range(2)]
+        z_s = [mx_tile("z_s%d" % h, U8, HALF) for h in range(2)]
+        a_ps = [psum.tile([P, S], F32, name="a_ps%d" % m, tag="ya%d" % m) for m in range(TILES)]
+        na = [keep.tile([P, S], F32, name="na%d" % m) for m in range(TILES)]
+        gated = [keep.tile([P, S], F32, name="gated%d" % m) for m in range(TILES)]
+        gain_b = gain[:].unsqueeze(1).unsqueeze(3).broadcast_to([P, HALF // 4, TILES, 4])
+
+        def pair(h, t):
+            nc.vector.tensor_tensor(hi[h][t][:], pa[h][t][:], pb[h][t][:], ALU.max)
+            nc.vector.tensor_tensor(lo[h][t][:], pa[h][t][:], pb[h][t][:], ALU.min)
+
+        def with_y(h, t):
+            nc.vector.tensor_tensor(hi[h][t][:], hi[h][t][:], y[t][:, cols(h)], ALU.max)
+            nc.vector.tensor_tensor(lo[h][t][:], lo[h][t][:], y[t][:, cols(h)], ALU.min)
+
+        def combine(h, t):
+            nc.vector.scalar_tensor_tensor(spread[h][:, t, :], lo[h][t][:], -0.5, hi[h][t][:], ALU.mult, ALU.add)
+
+        def apply_gain(h):
+            nc.vector.tensor_tensor(
+                z_bf[h][:].rearrange("p (c i t) -> p c t i", i=4, t=TILES),
+                spread[h][:].rearrange("p t (c i) -> p c t i", i=4),
+                gain_b,
+                ALU.mult,
+            )
+
+        def second_layer(h):
+            nc.vector.quantize_mx(z_w[h][:].bitcast(FP8X4), z_s[h][:], z_bf[h][:])
+            for m in range(TILES):
+                blk = slice(m * P, (m + 1) * P)
+                nc.tensor.matmul_mx(a_ps[m][:, cols(h)], w2_w[:, blk].bitcast(FP8X4), w2_s[:, blk], z_w[h][:].bitcast(FP8X4), z_s[h][:], start=True, stop=True)
+            for m in range(TILES):
+                nc.scalar.activation(na[m][:, cols(h)], a_ps[m][:, cols(h)], ACT.Copy, scale=-0.5)
+
+        def gate_it(h, m):
+            nc.vector.scalar_tensor_tensor(gated[m][:, cols(h)], gate[m][:, cols(h)], 1.0, na[m][:, cols(h)], ALU.add, ALU.mult)
+
+        units = [(h, t) for h in range(2) for t in range(TILES)]
+        for i, (h, t) in enumerate(units):
+            pair(h, t)
+            if i > 0:
+                combine(*units[i - 1])
+            with_y(h, t)
+            if (h, t) == (1, 0):
+                apply_gain(0)
+            if (h, t) == (1, 1):
+                second_layer(0)
+        gate_it(0, 0)
+        combine(1, TILES - 1)
+        gate_it(0, 1)
+        apply_gain(1)
+        gate_it(0, 2)
+        second_layer(1)
+        gate_it(0, 3)
+
+        res = [keep.tile([P, S], F32, name="res%d" % m) for m in range(TILES)]
+        far = [keep.tile([P, S], F32, name="far%d" % m) for m in range(1, TILES)]
+        for m in range(1, TILES):
+            for h in range(2):
+                nc.scalar.activation(far[m - 1][:, cols(h)], na[m][:].indirect(half_of(n3_t, h)), ACT.Copy)
+        gate_it(1, 0)
+        gate_it(1, 1)
+        for h in range(2):
+            nc.vector.tensor_tensor(res[0][:, cols(h)], na[0][:].indirect(half_of(n3_t, h)), gated[0][:, cols(h)], ALU.subtract)
+        nc.sync.dma_start(out[0:P, :], res[0][:])
+        gate_it(1, 2)
+        gate_it(1, 3)
+        for m in range(1, TILES):
+            nc.vector.tensor_tensor(res[m][:], far[m - 1][:], gated[m][:], ALU.subtract)
+            nc.sync.dma_start(out[m * P : (m + 1) * P, :], res[m][:])

@@ -18,6 +18,7 @@ S = 512
 TABLE = 2048
 HALF = S // 2
 TILES = 4
+WIDE = S + 16
 FLOPS = 3 * 2 * 512 * 512 * 512
 
 
@@ -41,8 +42,8 @@ def tile_picked_cdjoingatebrange_none_p_kernel(
         def cols(h):
             return slice(h * HALF, (h + 1) * HALF)
 
-        def mx_tile(name, dtype, width):
-            return keep.tile([P, width], dtype, name=name, align_bytes=64)
+        def mx_tile(name, dtype, width, tag=None):
+            return keep.tile([P, width], dtype, name=name, tag=tag or name, align_bytes=64)
 
         xw = mx_tile("xw", U32, TABLE)
         xs = mx_tile("xs", U8, TABLE)
@@ -50,28 +51,24 @@ def tile_picked_cdjoingatebrange_none_p_kernel(
         ds = mx_tile("ds", U8, TABLE)
         d_plane = mx_tile("d_plane", U8, S)
         nc.vector.memset(xs[:].bitcast(I32), 0)
-        nc.vector.memset(ds[:].bitcast(I32), 0)
-        nc.vector.memset(d_plane[:].bitcast(I32), 0)
+        nc.gpsimd.memset(ds[:].bitcast(I32), 0)
+        nc.gpsimd.memset(d_plane[:].bitcast(I32), 0)
 
         offs_t = load_list("offs_t", offs)
-        nc.sync.dma_start(xw[:].bitcast(I32), x_words[0].rearrange("p n t -> p (n t)").bitcast(I32))
-        for q in range(4):
-            nc.sync.dma_start(xs[32 * q : 32 * q + 4, :].bitcast(I32), x_scales[0, 4 * q : 4 * q + 4, :].bitcast(I32))
-        w1_rows = w1.rearrange("(p j) c -> p j c", j=PACK)
-        w1_raw = []
-        for h in range(2):
-            part = keep.tile([P, PACK, HALF], F32, name="w1_raw%d" % h)
-            nc.sync.dma_start(part[:], w1_rows[:, :, cols(h)])
-            w1_raw.append(part)
         two_t = load_list("two_t", two)
-        w2_raw = keep.tile([P, PACK, S], F32, name="w2_raw")
-        nc.sync.dma_start(w2_raw[:], w2.rearrange("(p j) c -> p j c", j=PACK))
-        n1_t = load_list("n1_t", n1)
-        n2_t = load_list("n2_t", n2)
+        for s in range(4):
+            nc.sync.dma_start(xs[s:P:32, :].bitcast(I32), x_scales[0, s:16:4, :].bitcast(I32))
+        nc.sync.dma_start(xw[:].bitcast(I32), x_words[0].rearrange("p n t -> p (n t)").bitcast(I32))
+        w1_raw = keep.tile([P, PACK, S], F32, name="w1_raw")
+        nc.sync.dma_start(w1_raw[:], w1.rearrange("(p j) c -> p j c", j=PACK))
         k1_t = load_list("k1_t", k1)
-        nc.sync.dma_start(dw[:].bitcast(I32), d_words[0].rearrange("p n t -> p (n t)").bitcast(I32))
         for e in range(2):
             nc.sync.dma_start(ds[e:P:16, :].bitcast(I32), d_scales[0, e:16:2, :].bitcast(I32))
+        n1_t = load_list("n1_t", n1)
+        n2_t = load_list("n2_t", n2)
+        nc.sync.dma_start(dw[:].bitcast(I32), d_words[0].rearrange("p n t -> p (n t)").bitcast(I32))
+        w2_raw = keep.tile([P, PACK, S], F32, name="w2_raw")
+        nc.sync.dma_start(w2_raw[:], w2.rearrange("(p j) c -> p j c", j=PACK))
         gain = keep.tile([P, PACK], F32, name="gain")
         nc.sync.dma_start(gain[:], gn.rearrange("(p t) o -> p (t o)", t=PACK))
         n4_t = load_list("n4_t", n4)
@@ -79,21 +76,18 @@ def tile_picked_cdjoingatebrange_none_p_kernel(
 
         xo_w = mx_tile("xo_w", U32, S)
         xo_s = mx_tile("xo_s", U8, S)
-        nc.vector.tensor_copy(xo_w[:], xw[:].indirect(offs_t[:]))
-        nc.vector.tensor_copy(xo_s[:], xs[:].indirect(offs_t[:]))
-
-        w1_bf = mx_tile("w1_bf", BF16, PACK * S)
-        w1_dealt = w1_bf[:].rearrange("p (t m j) -> p m j t", t=TILES, j=PACK)
-        for h in range(2):
-            nc.scalar.activation(
-                w1_dealt[:, 64 * h : 64 * (h + 1)],
-                w1_raw[h][:].rearrange("p j (m t) -> p m j t", t=TILES),
-                ACT.Copy,
-            )
-
         xt_w = mx_tile("xt_w", U32, S)
         xt_s = mx_tile("xt_s", U8, S)
+        nc.vector.tensor_copy(xo_s[:], xs[:].indirect(offs_t[:]))
+        nc.vector.tensor_copy(xt_s[:], xs[:].indirect(two_t[:]))
+        nc.vector.tensor_copy(xo_w[:], xw[:].indirect(offs_t[:]))
         nc.vector.tensor_copy(xt_w[:], xw[:].indirect(two_t[:]))
+
+        w1_bf = mx_tile("w1_bf", BF16, PACK * S)
+        w1_dealt = w1_bf[:].rearrange("p (u e m j) -> p u m j e", u=2, e=2, j=PACK)
+        w1_src = w1_raw[:].rearrange("p j (m u e) -> p u m j e", u=2, e=2)
+        nc.vector.tensor_copy(w1_dealt[:, 0], w1_src[:, 0])
+        nc.scalar.activation(w1_dealt[:, 1], w1_src[:, 1], ACT.Copy)
 
         w1_w = mx_tile("w1_w", U32, S)
         w1_s = mx_tile("w1_s", U8, S)
@@ -105,29 +99,21 @@ def tile_picked_cdjoingatebrange_none_p_kernel(
             nc.tensor.matmul_mx(bank[:], w1_w[:, blk].bitcast(FP8X4), w1_s[:, blk], xo_w[:].bitcast(FP8X4), xo_s[:], start=True, stop=True)
             y_ps.append(bank)
 
-        nc.vector.tensor_copy(xt_s[:], xs[:].indirect(two_t[:]))
 
-        y = [keep.tile([P, S], F32, name="y%d" % t) for t in range(TILES)]
-        pa = [[keep.tile([P, HALF], F32, name="pa%d_%d" % (h, t)) for t in range(TILES)] for h in range(2)]
-        pb = [[keep.tile([P, HALF], F32, name="pb%d_%d" % (h, t)) for t in range(TILES)] for h in range(2)]
-        for h in range(2):
-            for t in range(TILES):
-                if h == 0:
-                    nc.scalar.activation(y[t][:], y_ps[t][:], ACT.Copy)
-                nc.scalar.activation(pa[h][t][:], y[t][:].indirect(half_of(n1_t, h)), ACT.Copy)
-                nc.scalar.activation(pb[h][t][:], y[t][:].indirect(half_of(n2_t, h)), ACT.Copy)
+        y = [keep.tile([P, 2 * S], F32, name="y%d" % t) for t in range(TILES)]
+        pa = [keep.tile([P, S], F32, name="pa%d" % t) for t in range(TILES)]
+        pb = [keep.tile([P, S], F32, name="pb%d" % t) for t in range(TILES)]
+        for t in range(TILES):
+            nc.scalar.activation(y[t][:, 0:S], y_ps[t][:], ACT.Copy)
+            nc.scalar.activation(pa[t][:], y[t][:].indirect(n1_t[:]), ACT.Copy)
+            nc.scalar.activation(pb[t][:], y[t][:].indirect(n2_t[:]), ACT.Copy)
 
         w2_bf = mx_tile("w2_bf", BF16, PACK * S)
         w2_w = mx_tile("w2_w", U32, S)
         w2_s = mx_tile("w2_s", U8, S)
-        nc.vector.tensor_copy(
-            w2_bf[:].rearrange("p (c i j) -> p c j i", i=4, j=PACK),
-            w2_raw[:].rearrange("p j (c i) -> p c j i", i=4),
-        )
         dk_w = mx_tile("dk_w", U32, S)
-        dk_s = mx_tile("dk_s", U8, S)
+        dk_s = mx_tile("dk_s", U8, S, tag="w1_bf")
         nc.vector.tensor_copy(dk_s[:], ds[:].indirect(k1_t[:]))
-        nc.vector.quantize_mx(w2_w[:].bitcast(FP8X4), w2_s[:], w2_bf[:])
         nc.vector.tensor_copy(dk_w[:], dw[:].indirect(k1_t[:]))
         for s in range(4):
             src = 16 * (s // 2) + s % 2
@@ -138,84 +124,110 @@ def tile_picked_cdjoingatebrange_none_p_kernel(
             blk = slice(m * P, (m + 1) * P)
             bank = psum.tile([P, S], F32, name="b_ps%d" % m, tag="b%d" % m)
             nc.tensor.matmul_mx(bank[:], dk_w[:, blk].bitcast(FP8X4), d_plane[:, blk], xt_w[:].bitcast(FP8X4), xt_s[:], start=True, stop=True)
-            th = keep.tile([P, S], F32, name="th%d" % m)
-            nc.scalar.activation(th[:], bank[:], ACT.Tanh, scale=0.03125)
+            th = keep.tile([P, WIDE], F32, name="th%d" % m)
+            nc.scalar.activation(th[:, 0:S], bank[:], ACT.Tanh, scale=0.03125)
             g = keep.tile([P, S], F32, name="gate%d" % m)
-            for h in range(2):
-                nc.scalar.activation(g[:, cols(h)], th[:].indirect(half_of(n4_t, h)), ACT.Copy)
+            nc.scalar.activation(g[:], th[:].indirect(n4_t[:]), ACT.Copy, bias=0.5, scale=0.5)
             gate.append(g)
 
-        hi = [[keep.tile([P, HALF], F32, name="hi%d_%d" % (h, t)) for t in range(TILES)] for h in range(2)]
-        lo = [[keep.tile([P, HALF], F32, name="lo%d_%d" % (h, t)) for t in range(TILES)] for h in range(2)]
-        spread = [keep.tile([P, TILES, HALF], F32, name="spread%d" % h) for h in range(2)]
+        ring = keep.tile([P, 2, 2, S], F32, name="ring", tag="dw", align_bytes=64)
+        hi = [ring[:, t % 2, 0, :] for t in range(TILES)]
+        lo = [ring[:, t % 2, 1, :] for t in range(TILES)]
+        spread = keep.tile([P, TILES, S], F32, name="spread")
         z_bf = [mx_tile("z_bf%d" % h, BF16, PACK * HALF) for h in range(2)]
         z_w = [mx_tile("z_w%d" % h, U32, HALF) for h in range(2)]
         z_s = [mx_tile("z_s%d" % h, U8, HALF) for h in range(2)]
-        a_ps = [psum.tile([P, S], F32, name="a_ps%d" % m, tag="ya%d" % m) for m in range(TILES)]
-        na = [keep.tile([P, S], F32, name="na%d" % m) for m in range(TILES)]
+        a_ps = [[psum.tile([P, HALF], F32, name="a_ps%d_%d" % (h, m), tag=("ya%d", "b%d")[h] % m) for m in range(TILES)] for h in range(2)]
+        na = [keep.tile([P, WIDE], F32, name="na%d" % m) for m in range(TILES)]
         gated = [keep.tile([P, S], F32, name="gated%d" % m) for m in range(TILES)]
         gain_b = gain[:].unsqueeze(1).unsqueeze(3).broadcast_to([P, HALF // 4, TILES, 4])
+        every = slice(0, S)
 
-        def pair(h, t):
-            nc.vector.tensor_tensor(hi[h][t][:], pa[h][t][:], pb[h][t][:], ALU.max)
-            nc.vector.tensor_tensor(lo[h][t][:], pa[h][t][:], pb[h][t][:], ALU.min)
+        def with_pa(t):
+            nc.vector.tensor_tensor(hi[t], y[t][:, 0:S], pa[t][:], ALU.max)
+            nc.vector.tensor_tensor(lo[t], y[t][:, 0:S], pa[t][:], ALU.min)
 
-        def with_y(h, t):
-            nc.vector.tensor_tensor(hi[h][t][:], hi[h][t][:], y[t][:, cols(h)], ALU.max)
-            nc.vector.tensor_tensor(lo[h][t][:], lo[h][t][:], y[t][:, cols(h)], ALU.min)
+        def with_pb(ext, t, c, op):
+            nc.vector.tensor_tensor(ext[t][:, c], ext[t][:, c], pb[t][:, c], op)
 
-        def combine(h, t):
-            nc.vector.scalar_tensor_tensor(spread[h][:, t, :], lo[h][t][:], -0.5, hi[h][t][:], ALU.mult, ALU.add)
+        def combine(t, c):
+            nc.vector.scalar_tensor_tensor(spread[:, t, c], lo[t][:, c], -0.5, hi[t][:, c], ALU.mult, ALU.add)
 
         def apply_gain(h):
             nc.vector.tensor_tensor(
                 z_bf[h][:].rearrange("p (c i t) -> p c t i", i=4, t=TILES),
-                spread[h][:].rearrange("p t (c i) -> p c t i", i=4),
+                spread[:, :, cols(h)].rearrange("p t (c i) -> p c t i", i=4),
                 gain_b,
                 ALU.mult,
             )
 
-        def second_layer(h):
+        def quantise_z(h):
             nc.vector.quantize_mx(z_w[h][:].bitcast(FP8X4), z_s[h][:], z_bf[h][:])
-            for m in range(TILES):
-                blk = slice(m * P, (m + 1) * P)
-                nc.tensor.matmul_mx(a_ps[m][:, cols(h)], w2_w[:, blk].bitcast(FP8X4), w2_s[:, blk], z_w[h][:].bitcast(FP8X4), z_s[h][:], start=True, stop=True)
-            for m in range(TILES):
-                nc.scalar.activation(na[m][:, cols(h)], a_ps[m][:, cols(h)], ACT.Copy, scale=-0.5)
+
+        def second_layer(h, m):
+            blk = slice(m * P, (m + 1) * P)
+            nc.tensor.matmul_mx(a_ps[h][m][:], w2_w[:, blk].bitcast(FP8X4), w2_s[:, blk], z_w[h][:].bitcast(FP8X4), z_s[h][:], start=True, stop=True)
 
         def gate_it(h, m):
-            nc.vector.scalar_tensor_tensor(gated[m][:, cols(h)], gate[m][:, cols(h)], 1.0, na[m][:, cols(h)], ALU.add, ALU.mult)
+            nc.vector.tensor_tensor(gated[m][:, cols(h)], gate[m][:, cols(h)], a_ps[h][m][:], ALU.mult)
 
-        units = [(h, t) for h in range(2) for t in range(TILES)]
-        for i, (h, t) in enumerate(units):
-            pair(h, t)
-            if i > 0:
-                combine(*units[i - 1])
-            with_y(h, t)
-            if (h, t) == (1, 0):
-                apply_gain(0)
-            if (h, t) == (1, 1):
-                second_layer(0)
-        gate_it(0, 0)
-        combine(1, TILES - 1)
-        gate_it(0, 1)
+        def leave_bank(h, m):
+            nc.scalar.activation(na[m][:, cols(h)], a_ps[h][m][:], ACT.Copy, scale=-0.5)
+
+        last = TILES - 1
+        for t in range(TILES):
+            with_pa(t)
+            if t > 0:
+                combine(t - 1, every)
+            if t == 2:
+                nc.vector.quantize_mx(w2_w[:].bitcast(FP8X4), w2_s[:], w2_bf[:])
+            if t < last:
+                with_pb(hi, t, every, ALU.max)
+                with_pb(lo, t, every, ALU.min)
+            if t == 1:
+                nc.vector.tensor_copy(
+                    w2_bf[:].rearrange("p (c i j) -> p c j i", i=4, j=PACK),
+                    w2_raw[:].rearrange("p j (c i) -> p c j i", i=4),
+                )
+        with_pb(hi, last, cols(0), ALU.max)
+        with_pb(lo, last, cols(0), ALU.min)
+        with_pb(hi, last, cols(1), ALU.max)
+        combine(last, cols(0))
+        with_pb(lo, last, cols(1), ALU.min)
+        apply_gain(0)
+        combine(last, cols(1))
+        quantise_z(0)
+        for m in range(TILES):
+            second_layer(0, m)
         apply_gain(1)
-        gate_it(0, 2)
-        second_layer(1)
-        gate_it(0, 3)
+        gate_it(0, 0)
+        quantise_z(1)
+        for m in range(TILES):
+            second_layer(1, m)
+        for m in range(1, TILES):
+            gate_it(0, m)
+        for m in range(TILES):
+            leave_bank(0, m)
+        for m in range(TILES):
+            gate_it(1, m)
 
         res = [keep.tile([P, S], F32, name="res%d" % m) for m in range(TILES)]
-        far = [keep.tile([P, S], F32, name="far%d" % m) for m in range(1, TILES)]
-        for m in range(1, TILES):
-            for h in range(2):
-                nc.scalar.activation(far[m - 1][:, cols(h)], na[m][:].indirect(half_of(n3_t, h)), ACT.Copy)
-        gate_it(1, 0)
-        gate_it(1, 1)
-        for h in range(2):
-            nc.vector.tensor_tensor(res[0][:, cols(h)], na[0][:].indirect(half_of(n3_t, h)), gated[0][:, cols(h)], ALU.subtract)
-        nc.sync.dma_start(out[0:P, :], res[0][:])
-        gate_it(1, 2)
-        gate_it(1, 3)
-        for m in range(1, TILES):
-            nc.vector.tensor_tensor(res[m][:], far[m - 1][:], gated[m][:], ALU.subtract)
-            nc.sync.dma_start(out[m * P : (m + 1) * P, :], res[m][:])
+        far = [keep.tile([P, S], F32, name="far%d" % m) for m in range(2)]
+
+        def fetch(m, c, offsets):
+            nc.scalar.activation(far[m - 2][:, c], na[m][:].indirect(offsets), ACT.Copy)
+
+        def finish(m, c, fetched):
+            nc.vector.tensor_tensor(res[m][:, c], fetched, gated[m][:, c], ALU.add)
+            nc.sync.dma_start(out[m * P : (m + 1) * P, c], res[m][:, c])
+
+        for m in range(3):
+            leave_bank(1, m)
+        fetch(2, every, n3_t[:])
+        leave_bank(1, 3)
+        fetch(3, cols(1), half_of(n3_t, 1))
+        finish(0, every, na[0][:].indirect(n3_t[:]))
+        finish(2, every, far[0][:])
+        finish(1, every, na[1][:].indirect(n3_t[:]))
+        finish(3, cols(0), na[3][:].indirect(half_of(n3_t, 0)))
+        finish(3, cols(1), far[1][:, cols(1)])

@@ -19,6 +19,7 @@ TABLE = 2048
 HALF = S // 2
 TILES = 4
 WIDE = S + 16
+EARLY = 256
 FLOPS = 3 * 2 * 512 * 512 * 512
 
 
@@ -56,9 +57,11 @@ def tile_picked_cdjoingatebrange_none_p_kernel(
 
         offs_t = load_list("offs_t", offs)
         two_t = load_list("two_t", two)
+        x_flat = x_words[0].rearrange("p n t -> p (n t)").bitcast(I32)
+        nc.sync.dma_start(xw[:, 0:EARLY].bitcast(I32), x_flat[:, 0:EARLY])
         for s in range(4):
             nc.sync.dma_start(xs[s:P:32, :].bitcast(I32), x_scales[0, s:16:4, :].bitcast(I32))
-        nc.sync.dma_start(xw[:].bitcast(I32), x_words[0].rearrange("p n t -> p (n t)").bitcast(I32))
+        nc.sync.dma_start(xw[:, EARLY:TABLE].bitcast(I32), x_flat[:, EARLY:TABLE])
         w1_raw = keep.tile([P, PACK, S], F32, name="w1_raw")
         nc.sync.dma_start(w1_raw[:], w1.rearrange("(p j) c -> p j c", j=PACK))
         k1_t = load_list("k1_t", k1)
@@ -83,22 +86,35 @@ def tile_picked_cdjoingatebrange_none_p_kernel(
         nc.vector.tensor_copy(xo_w[:], xw[:].indirect(offs_t[:]))
         nc.vector.tensor_copy(xt_w[:], xw[:].indirect(two_t[:]))
 
-        w1_bf = mx_tile("w1_bf", BF16, PACK * S)
-        w1_dealt = w1_bf[:].rearrange("p (u e m j) -> p u m j e", u=2, e=2, j=PACK)
-        w1_src = w1_raw[:].rearrange("p j (m u e) -> p u m j e", u=2, e=2)
-        nc.vector.tensor_copy(w1_dealt[:, 0], w1_src[:, 0])
-        nc.scalar.activation(w1_dealt[:, 1], w1_src[:, 1], ACT.Copy)
+        w1_bf = [mx_tile("w1_bf%d" % u, BF16, 2 * S) for u in range(2)]
+        nc.vector.tensor_copy(
+            w1_bf[0][:].rearrange("p (e m j) -> p m j e", e=2, j=PACK),
+            w1_raw[:].rearrange("p j (m t) -> p m j t", t=TILES)[:, :, :, 0:2],
+        )
+        for e in range(2):
+            nc.scalar.activation(
+                w1_bf[1][:, e * S : (e + 1) * S].rearrange("p (m j) -> p m j", j=PACK),
+                w1_raw[:].rearrange("p j (m t) -> p t m j", t=TILES)[:, 2 + e],
+                ACT.Copy,
+            )
 
-        w1_w = mx_tile("w1_w", U32, S)
-        w1_s = mx_tile("w1_s", U8, S)
         y_ps = []
-        for t in range(TILES):
-            blk = slice(t * P, (t + 1) * P)
-            nc.vector.quantize_mx(w1_w[:, blk].bitcast(FP8X4), w1_s[:, blk], w1_bf[:, t * S : (t + 1) * S])
-            bank = psum.tile([P, S], F32, name="y_ps%d" % t, tag="ya%d" % t)
-            nc.tensor.matmul_mx(bank[:], w1_w[:, blk].bitcast(FP8X4), w1_s[:, blk], xo_w[:].bitcast(FP8X4), xo_s[:], start=True, stop=True)
-            y_ps.append(bank)
 
+        def first_layer(u, words_tag):
+            words = mx_tile("w1_w%d" % u, U32, 2 * P, tag=words_tag)
+            scales = mx_tile("w1_s%d" % u, U8, 2 * P)
+            for e in range(2):
+                t = 2 * u + e
+                blk = slice(e * P, (e + 1) * P)
+                nc.vector.quantize_mx(words[:, blk].bitcast(FP8X4), scales[:, blk], w1_bf[u][:, e * S : (e + 1) * S])
+                bank = psum.tile([P, S], F32, name="y_ps%d" % t, tag="ya%d" % t)
+                nc.tensor.matmul_mx(bank[:], words[:, blk].bitcast(FP8X4), scales[:, blk], xo_w[:].bitcast(FP8X4), xo_s[:], start=True, stop=True)
+                y_ps.append(bank)
+
+        first_layer(0, None)
+        dk_s = mx_tile("dk_s", U8, S, tag="w1_bf0")
+        nc.vector.tensor_copy(dk_s[:], ds[:].indirect(k1_t[:]))
+        first_layer(1, "ds")
 
         y = [keep.tile([P, 2 * S], F32, name="y%d" % t) for t in range(TILES)]
         pa = [keep.tile([P, S], F32, name="pa%d" % t) for t in range(TILES)]
@@ -112,8 +128,6 @@ def tile_picked_cdjoingatebrange_none_p_kernel(
         w2_w = mx_tile("w2_w", U32, S)
         w2_s = mx_tile("w2_s", U8, S)
         dk_w = mx_tile("dk_w", U32, S)
-        dk_s = mx_tile("dk_s", U8, S, tag="w1_bf")
-        nc.vector.tensor_copy(dk_s[:], ds[:].indirect(k1_t[:]))
         nc.vector.tensor_copy(dk_w[:], dw[:].indirect(k1_t[:]))
         for s in range(4):
             src = 16 * (s // 2) + s % 2
@@ -140,7 +154,7 @@ def tile_picked_cdjoingatebrange_none_p_kernel(
         a_ps = [[psum.tile([P, HALF], F32, name="a_ps%d_%d" % (h, m), tag=("ya%d", "b%d")[h] % m) for m in range(TILES)] for h in range(2)]
         na = [keep.tile([P, WIDE], F32, name="na%d" % m) for m in range(TILES)]
         gated = [keep.tile([P, S], F32, name="gated%d" % m) for m in range(TILES)]
-        gain_b = gain[:].unsqueeze(1).unsqueeze(3).broadcast_to([P, HALF // 4, TILES, 4])
+        gain_b = gain[:].unsqueeze(1).unsqueeze(3).broadcast_to([P, HALF // 2, TILES, 2])
         every = slice(0, S)
 
         def with_pa(t):
@@ -155,8 +169,8 @@ def tile_picked_cdjoingatebrange_none_p_kernel(
 
         def apply_gain(h):
             nc.vector.tensor_tensor(
-                z_bf[h][:].rearrange("p (c i t) -> p c t i", i=4, t=TILES),
-                spread[:, :, cols(h)].rearrange("p t (c i) -> p c t i", i=4),
+                z_bf[h][:].rearrange("p (c i t) -> p c t i", i=2, t=TILES),
+                spread[:, :, cols(h)].rearrange("p t (c i) -> p c t i", i=2),
                 gain_b,
                 ALU.mult,
             )
@@ -186,8 +200,8 @@ def tile_picked_cdjoingatebrange_none_p_kernel(
                 with_pb(lo, t, every, ALU.min)
             if t == 1:
                 nc.vector.tensor_copy(
-                    w2_bf[:].rearrange("p (c i j) -> p c j i", i=4, j=PACK),
-                    w2_raw[:].rearrange("p j (c i) -> p c j i", i=4),
+                    w2_bf[:].rearrange("p (c i j) -> p c j i", i=2, j=PACK),
+                    w2_raw[:].rearrange("p j (c i) -> p c j i", i=2),
                 )
         with_pb(hi, last, cols(0), ALU.max)
         with_pb(lo, last, cols(0), ALU.min)

from contextlib import ExitStack

import concourse.mybir as mybir

F32 = mybir.dt.float32
BF16 = mybir.dt.bfloat16
I32 = mybir.dt.int32
U32 = mybir.dt.uint32
U16 = mybir.dt.uint16
U8 = mybir.dt.uint8
FP8X4 = mybir.dt.float8_e4m3fn_x4
ACT = mybir.ActivationFunctionType
ALU = mybir.AluOpType

P = 128
PACK = 4
S = 512
TABLE = 2048
HALF = S // 2
TILES = 4
WIDE = S + 16
EARLY = 256
FLOPS = 3 * 2 * 512 * 512 * 512


def tile_picked_cdjoingatebrange_none_p_kernel(
    tc, x_words, x_scales, w1, gn, w2, d_words, d_scales, offs, n1, n2, two, k1, n3, n4, out
):
    nc = tc.nc
    with ExitStack() as ctx:
        lists = ctx.enter_context(tc.tile_pool(name="lists", bufs=1))
        keep = ctx.enter_context(tc.tile_pool(name="keep", bufs=1))
        psum = ctx.enter_context(tc.psum_pool(name="psum", bufs=1))

        def load_list(name, src):
            tile = lists.tile([P, S // 16], U16, name=name)
            nc.sync.dma_start(tile[:], src)
            return tile

        def half_of(list_tile, h):
            return list_tile[:, h * (HALF // 16) : (h + 1) * (HALF // 16)]

        def cols(h):
            return slice(h * HALF, (h + 1) * HALF)

        def mx_tile(name, dtype, width, tag=None):
            return keep.tile([P, width], dtype, name=name, tag=tag or name, align_bytes=64)

        xw = mx_tile("xw", U32, TABLE)
        xs = mx_tile("xs", U8, TABLE)
        dw = mx_tile("dw", U32, TABLE)
        ds = mx_tile("ds", U8, TABLE)
        d_plane = mx_tile("d_plane", U8, S)
        nc.vector.memset(xs[:].bitcast(I32), 0)
        nc.gpsimd.memset(ds[:].bitcast(I32), 0)
        nc.gpsimd.memset(d_plane[:].bitcast(I32), 0)

        offs_t = load_list("offs_t", offs)
        two_t = load_list("two_t", two)
        x_flat = x_words[0].rearrange("p n t -> p (n t)").bitcast(I32)
        nc.sync.dma_start(xw[:, 0:EARLY].bitcast(I32), x_flat[:, 0:EARLY])
        for s in range(4):
            nc.sync.dma_start(xs[s:P:32, :].bitcast(I32), x_scales[0, s:16:4, :].bitcast(I32))
        nc.sync.dma_start(xw[:, EARLY:TABLE].bitcast(I32), x_flat[:, EARLY:TABLE])
        w1_raw = keep.tile([P, PACK, S], F32, name="w1_raw")
        nc.sync.dma_start(w1_raw[:], w1.rearrange("(p j) c -> p j c", j=PACK))
        k1_t = load_list("k1_t", k1)
        for e in range(2):
            nc.sync.dma_start(ds[e:P:16, :].bitcast(I32), d_scales[0, e:16:2, :].bitcast(I32))
        n1_t = load_list("n1_t", n1)
        n2_t = load_list("n2_t", n2)
        nc.sync.dma_start(dw[:].bitcast(I32), d_words[0].rearrange("p n t -> p (n t)").bitcast(I32))
        w2_raw = keep.tile([P, PACK, S], F32, name="w2_raw")
        nc.sync.dma_start(w2_raw[:], w2.rearrange("(p j) c -> p j c", j=PACK))
        gain = keep.tile([P, PACK], F32, name="gain")
        nc.sync.dma_start(gain[:], gn.rearrange("(p t) o -> p (t o)", t=PACK))
        n4_t = load_list("n4_t", n4)
        n3_t = load_list("n3_t", n3)

        xo_w = mx_tile("xo_w", U32, S)
        xo_s = mx_tile("xo_s", U8, S)
        xt_w = mx_tile("xt_w", U32, S)
        xt_s = mx_tile("xt_s", U8, S)
        nc.vector.tensor_copy(xo_s[:], xs[:].indirect(offs_t[:]))
        nc.vector.tensor_copy(xt_s[:], xs[:].indirect(two_t[:]))
        nc.vector.tensor_copy(xo_w[:], xw[:].indirect(offs_t[:]))
        nc.vector.tensor_copy(xt_w[:], xw[:].indirect(two_t[:]))

        w1_bf = [mx_tile("w1_bf%d" % u, BF16, 2 * S) for u in range(2)]
        nc.vector.tensor_copy(
            w1_bf[0][:].rearrange("p (e m j) -> p m j e", e=2, j=PACK),
            w1_raw[:].rearrange("p j (m t) -> p m j t", t=TILES)[:, :, :, 0:2],
        )
        for e in range(2):
            nc.scalar.activation(
                w1_bf[1][:, e * S : (e + 1) * S].rearrange("p (m j) -> p m j", j=PACK),
                w1_raw[:].rearrange("p j (m t) -> p t m j", t=TILES)[:, 2 + e],
                ACT.Copy,
            )

        y_ps = []

        def first_layer(u, words_tag):
            words = mx_tile("w1_w%d" % u, U32, 2 * P, tag=words_tag)
            scales = mx_tile("w1_s%d" % u, U8, 2 * P)
            for e in range(2):
                t = 2 * u + e
                blk = slice(e * P, (e + 1) * P)
                nc.vector.quantize_mx(words[:, blk].bitcast(FP8X4), scales[:, blk], w1_bf[u][:, e * S : (e + 1) * S])
                bank = psum.tile([P, S], F32, name="y_ps%d" % t, tag="ya%d" % t)
                nc.tensor.matmul_mx(bank[:], words[:, blk].bitcast(FP8X4), scales[:, blk], xo_w[:].bitcast(FP8X4), xo_s[:], start=True, stop=True)
                y_ps.append(bank)

        first_layer(0, None)
        dk_s = mx_tile("dk_s", U8, S, tag="w1_bf0")
        nc.vector.tensor_copy(dk_s[:], ds[:].indirect(k1_t[:]))
        first_layer(1, "ds")

        y = [keep.tile([P, 2 * S], F32, name="y%d" % t) for t in range(TILES)]
        pa = [keep.tile([P, S], F32, name="pa%d" % t) for t in range(TILES)]
        pb = [keep.tile([P, S], F32, name="pb%d" % t) for t in range(TILES)]
        for t in range(TILES):
            nc.scalar.activation(y[t][:, 0:S], y_ps[t][:], ACT.Copy)
            nc.scalar.activation(pa[t][:], y[t][:].indirect(n1_t[:]), ACT.Copy)
            nc.scalar.activation(pb[t][:], y[t][:].indirect(n2_t[:]), ACT.Copy)

        w2_bf = mx_tile("w2_bf", BF16, PACK * S)
        w2_w = mx_tile("w2_w", U32, S)
        w2_s = mx_tile("w2_s", U8, S)
        dk_w = mx_tile("dk_w", U32, S)
        nc.vector.tensor_copy(dk_w[:], dw[:].indirect(k1_t[:]))
        for s in range(4):
            src = 16 * (s // 2) + s % 2
            nc.sync.dma_start(d_plane[s:P:32, :].bitcast(I32), dk_s[src:P:32, :].bitcast(I32))

        gate = []
        for m in range(TILES):
            blk = slice(m * P, (m + 1) * P)
            bank = psum.tile([P, S], F32, name="b_ps%d" % m, tag="b%d" % m)
            nc.tensor.matmul_mx(bank[:], dk_w[:, blk].bitcast(FP8X4), d_plane[:, blk], xt_w[:].bitcast(FP8X4), xt_s[:], start=True, stop=True)
            th = keep.tile([P, WIDE], F32, name="th%d" % m)
            nc.scalar.activation(th[:, 0:S], bank[:], ACT.Tanh, scale=0.03125)
            g = keep.tile([P, S], F32, name="gate%d" % m)
            nc.scalar.activation(g[:], th[:].indirect(n4_t[:]), ACT.Copy, bias=0.5, scale=0.5)
            gate.append(g)

        ring = keep.tile([P, 2, 2, S], F32, name="ring", tag="dw", align_bytes=64)
        hi = [ring[:, t % 2, 0, :] for t in range(TILES)]
        lo = [ring[:, t % 2, 1, :] for t in range(TILES)]
        spread = keep.tile([P, TILES, S], F32, name="spread")
        z_bf = [mx_tile("z_bf%d" % h, BF16, PACK * HALF) for h in range(2)]
        z_w = [mx_tile("z_w%d" % h, U32, HALF) for h in range(2)]
        z_s = [mx_tile("z_s%d" % h, U8, HALF) for h in range(2)]
        a_ps = [[psum.tile([P, HALF], F32, name="a_ps%d_%d" % (h, m), tag=("ya%d", "b%d")[h] % m) for m in range(TILES)] for h in range(2)]
        na = [keep.tile([P, WIDE], F32, name="na%d" % m) for m in range(TILES)]
        gated = [keep.tile([P, S], F32, name="gated%d" % m) for m in range(TILES)]
        gain_b = gain[:].unsqueeze(1).unsqueeze(3).broadcast_to([P, HALF // 2, TILES, 2])
        every = slice(0, S)

        def with_pa(t):
            nc.vector.tensor_tensor(hi[t], y[t][:, 0:S], pa[t][:], ALU.max)
            nc.vector.tensor_tensor(lo[t], y[t][:, 0:S], pa[t][:], ALU.min)

        def with_pb(ext, t, c, op):
            nc.vector.tensor_tensor(ext[t][:, c], ext[t][:, c], pb[t][:, c], op)

        def combine(t, c):
            nc.vector.scalar_tensor_tensor(spread[:, t, c], lo[t][:, c], -0.5, hi[t][:, c], ALU.mult, ALU.add)

        def apply_gain(h):
            nc.vector.tensor_tensor(
                z_bf[h][:].rearrange("p (c i t) -> p c t i", i=2, t=TILES),
                spread[:, :, cols(h)].rearrange("p t (c i) -> p c t i", i=2),
                gain_b,
                ALU.mult,
            )

        def quantise_z(h):
            nc.vector.quantize_mx(z_w[h][:].bitcast(FP8X4), z_s[h][:], z_bf[h][:])

        def second_layer(h, m):
            blk = slice(m * P, (m + 1) * P)
            nc.tensor.matmul_mx(a_ps[h][m][:], w2_w[:, blk].bitcast(FP8X4), w2_s[:, blk], z_w[h][:].bitcast(FP8X4), z_s[h][:], start=True, stop=True)

        def gate_it(h, m):
            nc.vector.tensor_tensor(gated[m][:, cols(h)], gate[m][:, cols(h)], a_ps[h][m][:], ALU.mult)

        def leave_bank(h, m):
            nc.scalar.activation(na[m][:, cols(h)], a_ps[h][m][:], ACT.Copy, scale=-0.5)

        last = TILES - 1
        for t in range(TILES):
            with_pa(t)
            if t > 0:
                combine(t - 1, every)
            if t == 2:
                nc.vector.quantize_mx(w2_w[:].bitcast(FP8X4), w2_s[:], w2_bf[:])
            if t < last:
                with_pb(hi, t, every, ALU.max)
                with_pb(lo, t, every, ALU.min)
            if t == 1:
                nc.vector.tensor_copy(
                    w2_bf[:].rearrange("p (c i j) -> p c j i", i=2, j=PACK),
                    w2_raw[:].rearrange("p j (c i) -> p c j i", i=2),
                )
        with_pb(hi, last, cols(0), ALU.max)
        with_pb(lo, last, cols(0), ALU.min)
        with_pb(hi, last, cols(1), ALU.max)
        combine(last, cols(0))
        with_pb(lo, last, cols(1), ALU.min)
        apply_gain(0)
        combine(last, cols(1))
        quantise_z(0)
        for m in range(TILES):
            second_layer(0, m)
        apply_gain(1)
        gate_it(0, 0)
        quantise_z(1)
        for m in range(TILES):
            second_layer(1, m)
        for m in range(1, TILES):
            gate_it(0, m)
        for m in range(TILES):
            leave_bank(0, m)
        for m in range(TILES):
            gate_it(1, m)

        res = [keep.tile([P, S], F32, name="res%d" % m) for m in range(TILES)]
        far = [keep.tile([P, S], F32, name="far%d" % m) for m in range(2)]

        def fetch(m, c, offsets):
            nc.scalar.activation(far[m - 2][:, c], na[m][:].indirect(offsets), ACT.Copy)

        def finish(m, c, fetched):
            nc.vector.tensor_tensor(res[m][:, c], fetched, gated[m][:, c], ALU.add)
            nc.sync.dma_start(out[m * P : (m + 1) * P, c], res[m][:, c])

        for m in range(3):
            leave_bank(1, m)
        fetch(2, every, n3_t[:])
        leave_bank(1, 3)
        fetch(3, cols(1), half_of(n3_t, 1))
        finish(0, every, na[0][:].indirect(n3_t[:]))
        finish(2, every, far[0][:])
        finish(1, every, na[1][:].indirect(n3_t[:]))
        finish(3, cols(0), na[3][:].indirect(half_of(n3_t, 0)))
        finish(3, cols(1), far[1][:, cols(1)])
